import numpy as np
import ml_dtypes


def mxq(x, axis, fmt="e4m3"):
    dtype, down = {"e4m3": (ml_dtypes.float8_e4m3fn, 7), "e5m2": (ml_dtypes.float8_e5m2, 14)}[fmt]
    v = np.moveaxis(np.asarray(x, np.float32).astype(ml_dtypes.bfloat16).astype(np.float64), axis, -1)
    blocks = v.reshape(v.shape[:-1] + (-1, 32))
    amax = np.abs(blocks).max(-1, keepdims=True)
    byte = np.maximum(np.where(amax > 0, np.frexp(amax)[1] - 1 + 127, 0) - down, 1)
    scale = np.exp2(byte - 127.0)
    codes = (blocks / scale).astype(np.float32).astype(dtype).astype(np.float64)
    return np.moveaxis((codes * scale).reshape(v.shape), -1, axis)


WIDE = False


def mx_kscale(k):
    if not WIDE:
        return np.ones(k)
    levels = np.array([10, -10, 5, -5, 0])
    if k % 512:
        return np.exp2(np.random.permutation(np.resize(levels, k // 32))).repeat(32)
    a = np.empty((k // 512, 16))
    for p in range(k // 512):
        a[p, :8] = np.random.permutation(np.resize(levels, 8))
        for g in range(8):
            far = levels[np.abs(levels - a[p, g]) >= 10]
            a[p, g + 8] = far[np.random.randint(len(far))]
    return np.exp2(a.ravel()).repeat(32)


def f64(x):
    return np.asarray(x).astype(np.float64)


def striped(idx):
    return np.tile(idx.reshape(-1, 16).T, (8, 1)).astype(np.uint16)


def unstriped(offs):
    return offs[:16].T.reshape(-1).astype(np.int64)


def striped8(idx):
    return np.concatenate([x.reshape(-1, 16).T for x in idx]).astype(np.uint16)


def runs(offs, k):
    lists = np.stack([offs[16 * r : 16 * r + 16].T.reshape(-1) for r in range(8)]).astype(np.int64)
    return lists[np.arange(k) % 512 // 64]


def pack_weight(w):
    k, n = w.shape
    w = f64(np.asarray(w, np.float32).astype(ml_dtypes.bfloat16)).reshape(k // 32, 32, n)
    amax = np.abs(w).max(1)
    byte = np.clip(np.where(amax > 0, np.frexp(amax)[1] - 1 + 127 - 7, 1), 1, 254)
    scaled = (w * np.exp2(127.0 - byte)[:, None, :]).reshape(k, n).astype(np.float32)
    words = np.ascontiguousarray(scaled.reshape(k // 512, 128, 4, n).transpose(0, 1, 3, 2)).astype(ml_dtypes.float8_e4m3fn).view(np.uint8)
    return words, np.ascontiguousarray(byte.astype(np.uint8).reshape(k // 512, 16, n))


def unpack_weight(words, scales):
    g, p, n, _ = words.shape
    vals = np.ascontiguousarray(words).view(ml_dtypes.float8_e4m3fn).astype(np.float64) * np.repeat(np.exp2(scales.astype(np.float64) - 127.0), 8, axis=1)[..., None]
    return vals.transpose(0, 1, 3, 2).reshape(g * 512, n)


E2M1 = np.array([0.0, 0.5, 1.0, 1.5, 2.0, 3.0, 4.0, 6.0, -0.0, -0.5, -1.0, -1.5, -2.0, -3.0, -4.0, -6.0])


def pack_fp4(w):
    k, n = w.shape
    w = f64(np.asarray(w, np.float32).astype(ml_dtypes.bfloat16)).reshape(k // 32, 32, n)
    amax = np.abs(w).max(1)
    mant, ex = np.frexp(amax / 6.0)
    byte = np.clip(np.where(amax > 0, np.where(mant > 0.5, ex, ex - 1) + 127, 1), 1, 254)
    scaled = (w * np.exp2(127.0 - byte)[:, None, :]).reshape(k, n).astype(np.float32)
    c = np.ascontiguousarray(scaled.reshape(k // 512, 128, 4, n).transpose(0, 1, 3, 2)).astype(ml_dtypes.float4_e2m1fn).view(np.uint8) & 0xF
    words = (c[..., 0::2] | (c[..., 1::2] << 4)).reshape(k // 512, 128, 2 * n)
    return np.ascontiguousarray(words), np.ascontiguousarray(byte.astype(np.uint8).reshape(k // 512, 16, n))


def unpack_fp4(words, scales):
    g, _, n = scales.shape
    words = np.ascontiguousarray(words).reshape(g, 128, n, 2)
    nib = np.empty((g, 128, n, 4), np.uint8)
    nib[..., 0::2] = words & 0xF
    nib[..., 1::2] = words >> 4
    vals = E2M1[nib] * np.repeat(np.exp2(scales.astype(np.float64) - 127.0), 8, axis=1)[..., None]
    return vals.transpose(0, 1, 3, 2).reshape(g * 512, n)


def planes(y):
    n, m = y.shape
    v = y.astype(np.float32).astype(ml_dtypes.bfloat16).astype(np.float64).reshape(n // 32, 32, m)
    top = np.abs(v).max(1)
    byte = np.clip(np.where(top > 0, np.frexp(top)[1] - 1 + 127 - 7, 1), 1, 254)
    codes = (v * np.exp2(127.0 - byte)[:, None, :]).reshape(n, m).astype(np.float32).astype(ml_dtypes.float8_e4m3fn).view(np.uint8)
    words = codes.reshape(n // 512, 128, 4, m).transpose(0, 1, 3, 2)
    return np.ascontiguousarray(words), np.ascontiguousarray(byte.astype(np.uint8).reshape(n // 512, 16, m))


K, T, S, H, W, C = 512, 2048, 512, 512, 256, 512


def setup_inputs():
    n = np.random.standard_normal
    s = mx_kscale(K)[:, None]
    packed_xT = pack_weight(n((K, T)) * s)
    packed_w1 = pack_fp4(n((K, H)) / np.sqrt(K) / s)
    perm = np.stack([np.random.permutation(S) for _ in range(8)])
    return {
        "x_words": packed_xT[0],
        "x_scales": packed_xT[1],
        "w1_words": packed_w1[0],
        "w1_scales": packed_w1[1],
        "gs": (np.random.uniform(0.5, 1.5, (K, 1)) / s).astype(np.float32),
        "offs": striped(np.random.permutation(T)[:S]),
        "n1": striped8(perm[:, :W]),
        "n2": striped8(perm[:, W:]),
        "n3": striped8(np.stack([np.random.permutation(S) for _ in range(8)])),
        "ca": striped(np.random.permutation(T)[:C]),
        "cb": striped(np.random.permutation(T)[:C]),
        "n4": striped8(np.stack([np.random.permutation(S) for _ in range(8)])),
        "n5": striped8(np.stack([np.random.permutation(S) for _ in range(8)])),
        "n6": striped8(np.stack([np.random.permutation(S) for _ in range(8)])),
        "n7": striped8(np.stack([np.random.permutation(S) for _ in range(8)])),
    }


def reference(x_words, x_scales, w1_words, w1_scales, gs, offs, n1, n2, n3, ca, cb, n4, n5, n6, n7):
    x_ca = unpack_weight(x_words, x_scales)[:, unstriped(ca)]
    xq = unpack_weight(x_words, x_scales)[:, unstriped(offs)]
    y = unpack_fp4(w1_words, w1_scales).T @ xq
    pa = y[np.arange(H)[:, None], runs(n1, H)]
    pb = y[np.arange(H)[:, None], runs(n2, H)]
    ra = pa - (0.5 * pb)
    ds = y.copy()
    ds[np.arange(H)[:, None], runs(n2, H)] = ra
    z = f64(gs) * (ds - (0.5 * (ds[np.arange(H)[:, None], runs(n3, H)])))
    zq = mxq(z, 0, "e4m3")
    a = 0.0625 * (x_ca.T @ zq)
    x_cb = unpack_weight(x_words, x_scales)[:, unstriped(cb)]
    b = 0.0625 * (x_cb.T @ zq)
    out_0 = np.maximum(a[np.arange(C)[:, None], runs(n4, C)] + b[np.arange(C)[:, None], runs(n6, C)], a[np.arange(C)[:, None], runs(n5, C)] + b[np.arange(C)[:, None], runs(n7, C)])
    return (out_0,) + planes(out_0)

@@ -1,0 +1,194 @@
+from contextlib import ExitStack
+
+import concourse.mybir as mybir
+
+F32 = mybir.dt.float32
+BF16 = mybir.dt.bfloat16
+I32 = mybir.dt.int32
+U32 = mybir.dt.uint32
+U16 = mybir.dt.uint16
+U8 = mybir.dt.uint8
+FP8X4 = mybir.dt.float8_e4m3fn_x4
+FP4X4 = mybir.dt.float4_e2m1fn_x4
+ALU = mybir.AluOpType
+COPY = mybir.ActivationFunctionType.Copy
+
+P = 128
+PACK = 4
+T = 2048
+S = 512
+W = 256
+WIN = 2 * S
+FLOPS = 3 * 2 * 512 * 512 * 512
+
+
+def tile_picked_ccmppathbfoldd_none_po_kernel(
+    tc, x_words, x_scales, w1_words, w1_scales, gs, offs, n1, n2, n3, ca, cb, n4, n5, n6, n7, out_0, out_1, out_2
+):
+    nc = tc.nc
+    with ExitStack() as ctx:
+        lists = ctx.enter_context(tc.tile_pool(name="lists", bufs=1))
+        keep = ctx.enter_context(tc.tile_pool(name="keep", bufs=1))
+        ring = ctx.enter_context(tc.tile_pool(name="ring", bufs=2))
+        psum = ctx.enter_context(tc.psum_pool(name="psum", bufs=8))
+
+        def load_list(name, src):
+            t = lists.tile([P, src.shape[1]], U16, name=name)
+            nc.sync.dma_start(t[:], src)
+            return t
+
+        def load_scale_rows(queue, plane, src):
+            for q in range(4):
+                queue.dma_start(plane[32 * q : 32 * q + 4, :].bitcast(I32), src[0, 4 * q : 4 * q + 4, :].bitcast(I32))
+
+        xs = keep.tile([P, T], U8, name="xs", align_bytes=64)
+        ws = keep.tile([P, S], U8, name="ws", tag="ws", align_bytes=64)
+        nc.vector.memset(xs[:].bitcast(I32), 0)
+        nc.vector.memset(ws[:].bitcast(I32), 0)
+        l_offs = load_list("l_offs", offs)
+        ww = keep.tile([P, 2 * S], U8, name="ww", tag="ww", align_bytes=64)
+        nc.sync.dma_start(ww[:].bitcast(I32), w1_words[0].bitcast(I32))
+        load_scale_rows(nc.sync, xs, x_scales)
+        xw = keep.tile([P, T], U32, name="xw", align_bytes=64)
+        nc.sync.dma_start(xw[:].bitcast(I32), x_words[0].rearrange("p n r -> p (n r)").bitcast(I32))
+        l_ca = load_list("l_ca", ca)
+        load_scale_rows(nc.sync, ws, w1_scales)
+        l1 = load_list("l1", n1)
+        l2 = load_list("l2", n2)
+        l3 = load_list("l3", n3)
+        gain = keep.tile([P, PACK], F32, name="gain")
+        nc.sync.dma_start(gain[:], gs.rearrange("(p t) o -> p (t o)", t=PACK))
+        l_cb = load_list("l_cb", cb)
+        l4 = load_list("l4", n4)
+        l5 = load_list("l5", n5)
+        l6 = load_list("l6", n6)
+        l7 = load_list("l7", n7)
+
+        ds = [keep.tile([P, WIN], F32, name="ds%d" % t, tag="ds%d" % t, align_bytes=64) for t in range(PACK)]
+        for t in range(PACK):
+            nc.vector.memset(ds[t][:, S:], 0.0)
+        aw = [keep.tile([P, WIN], F32, name="aw%d" % t, align_bytes=64) for t in range(PACK)]
+        bw = [keep.tile([P, WIN], F32, name="bw%d" % t, align_bytes=64) for t in range(PACK)]
+
+        def deal_words(name, src):
+            dst = keep.tile([P, S], U32, name=name, align_bytes=64)
+            nc.vector.tensor_copy(
+                dst[:].rearrange("p (t g i) -> p g t i", t=PACK, i=4), src[:].rearrange("p (g i t) -> p g t i", t=PACK, i=4)
+            )
+            return dst
+
+        def deal_bytes(name, src):
+            dst = keep.tile([P, S], U8, name=name, align_bytes=64)
+            nc.vector.tensor_copy(dst[:].rearrange("p (t m) -> p t m", t=PACK), src[:].rearrange("p (m t) -> p t m", t=PACK))
+            return dst
+
+        def gather(name, table, dtype, offsets, tag):
+            dst = keep.tile([P, S], dtype, name=name, tag=tag, align_bytes=64)
+            nc.vector.tensor_copy(dst[:], table[:].indirect(offsets[:]))
+            return dst
+
+        qs = gather("qs", xs, U8, l_offs, "qs")
+        wwd = keep.tile([P, 2 * S], U8, name="wwd", align_bytes=64)
+        nc.vector.tensor_copy(
+            wwd[:].rearrange("p (t m b) -> p t m b", t=PACK, b=2), ww[:].rearrange("p (m t b) -> p t m b", t=PACK, b=2)
+        )
+        cas = gather("cas", xs, U8, l_ca, "ww")
+        qw = gather("qw", xw, U32, l_offs, "qw")
+        wsd = deal_bytes("wsd", ws)
+        caw = gather("caw", xw, U32, l_ca, "ws")
+        casd = deal_bytes("casd", cas)
+        cawd = deal_words("cawd", caw)
+
+        factor = keep.tile([P, PACK], F32, name="factor")
+        nc.scalar.activation(factor[:], gain[:], COPY, scale=-0.5)
+
+        for t in range(PACK):
+            acc = psum.tile([P, S], F32, name="acc")
+            nc.tensor.matmul_mx(
+                out=acc[:],
+                lhsT=wwd[:, 2 * P * t : 2 * P * (t + 1)].bitcast(FP4X4),
+                lhsT_scale=wsd[:, P * t : P * (t + 1)],
+                rhs=qw[:].bitcast(FP8X4),
+                rhs_scale=qs[:],
+                start=True,
+                stop=True,
+            )
+            nc.scalar.copy(ds[t][:, :S], acc[:])
+
+        zb = keep.tile([P, S, PACK], BF16, name="zb", tag="zb", align_bytes=64)
+
+        def mix(t):
+            nc.vector.tensor_tensor(aw[t][:, S:], ds[t][:].indirect(l3[:]), bw[t][:, S:], ALU.subtract)
+            nc.scalar.activation(zb[:, :, t], aw[t][:, S:], COPY, scale=factor[:, t : t + 1])
+
+        for t in range(PACK):
+            pa = ring.tile([P, W], F32, name="pa")
+            pb = ring.tile([P, W], F32, name="pb")
+            nc.vector.tensor_copy(pa[:], ds[t][:].indirect(l1[:]))
+            nc.vector.tensor_scalar(pb[:], ds[t][:].indirect(l2[:]), -0.5, 0.0, ALU.mult, ALU.add)
+            if t > 0:
+                mix(t - 1)
+            nc.vector.tensor_tensor(ds[t][:].indirect(l2[:]), pa[:], pb[:], ALU.add)
+            nc.scalar.activation(bw[t][:, S:], ds[t][:, :S], COPY, scale=2.0)
+        mix(PACK - 1)
+
+        cbw = gather("cbw", xw, U32, l_cb, "ds%d" % (PACK - 1))
+        cbwd = deal_words("cbwd", cbw)
+        zw = keep.tile([P, S], U32, name="zw", align_bytes=64)
+        zs = keep.tile([P, S], U8, name="zs", align_bytes=64)
+        nc.vector.quantize_mx(out=zw[:].bitcast(FP8X4), scales=zs[:], in_=zb[:].rearrange("p c t -> p (c t)"))
+        cbs = gather("cbs", xs, U8, l_cb, "zb")
+        cbsd = deal_bytes("cbsd", cbs)
+
+        for t in range(PACK):
+            for words, scales, window in ((cawd, casd, aw[t]), (cbwd, cbsd, bw[t])):
+                acc = psum.tile([P, S], F32, name="acc")
+                nc.tensor.matmul_mx(
+                    out=acc[:],
+                    lhsT=words[:, P * t : P * (t + 1)].bitcast(FP8X4),
+                    lhsT_scale=scales[:, P * t : P * (t + 1)],
+                    rhs=zw[:].bitcast(FP8X4),
+                    rhs_scale=zs[:],
+                    start=True,
+                    stop=True,
+                )
+                nc.scalar.activation(window[:, :S], acc[:], COPY, scale=0.0625)
+
+        ob = keep.tile([P, S, PACK], BF16, name="ob", align_bytes=64)
+        ow = keep.tile([P, S], U32, name="ow", align_bytes=64)
+        osc = keep.tile([P, S], U8, name="osc", align_bytes=64)
+        out_rows = out_0.rearrange("(p t) c -> p t c", t=PACK)
+        out_words = out_1[0].rearrange("p c r -> p (c r)").bitcast(I32)
+
+        def finish(t, c0, c1, s1, s2):
+            n = c1 - c0
+            res = ring.tile([P, S], F32, name="res", bufs=3)
+            nc.vector.tensor_tensor(res[:, :n], s1[:, :n], s2[:, :n], ALU.max)
+            nc.scalar.copy(ob[:, c0:c1, t], res[:, :n])
+            nc.sync.dma_start(out_rows[:, t, c0:c1], res[:, :n])
+            if t == PACK - 1:
+                nc.vector.quantize_mx(
+                    out=ow[:, c0:c1].bitcast(FP8X4), scales=osc[:, c0:c1], in_=ob[:, c0:c1, :].rearrange("p c t -> p (c t)")
+                )
+                nc.sync.dma_start(out_words[:, c0:c1], ow[:, c0:c1].bitcast(I32))
+
+        pieces = [(t, 0, S) for t in range(PACK - 1)] + [(PACK - 1, 0, W), (PACK - 1, W, S)]
+        pending = None
+        for t, c0, c1 in pieces:
+            n = c1 - c0
+            cols = slice(c0 // 16, c1 // 16)
+            g4 = ring.tile([P, S], F32, name="g4")
+            g5 = ring.tile([P, S], F32, name="g5")
+            s1 = ring.tile([P, S], F32, name="s1")
+            s2 = ring.tile([P, S], F32, name="s2")
+            nc.vector.tensor_copy(g4[:, :n], aw[t][:].indirect(l4[:, cols]))
+            if pending is not None:
+                finish(*pending)
+            nc.vector.tensor_copy(g5[:, :n], aw[t][:].indirect(l5[:, cols]))
+            nc.vector.tensor_tensor(s1[:, :n], bw[t][:].indirect(l6[:, cols]), g4[:, :n], ALU.add)
+            nc.vector.tensor_tensor(s2[:, :n], bw[t][:].indirect(l7[:, cols]), g5[:, :n], ALU.add)
+            pending = (t, c0, c1, s1, s2)
+        finish(*pending)
+        for q in range(4):
+            queue = nc.scalar if q % 2 else nc.sync
+            queue.dma_start(out_2[0, 4 * q : 4 * q + 4, :].bitcast(I32), osc[32 * q : 32 * q + 4, :].bitcast(I32))

@@ -29,6 +29,7 @@ def tile_picked_ccmppathbfoldd_none_po_kernel(
     with ExitStack() as ctx:
         lists = ctx.enter_context(tc.tile_pool(name="lists", bufs=1))
         keep = ctx.enter_context(tc.tile_pool(name="keep", bufs=1))
+        reuse = ctx.enter_context(tc.tile_pool(name="reuse", bufs=1))
         ring = ctx.enter_context(tc.tile_pool(name="ring", bufs=2))
         psum = ctx.enter_context(tc.psum_pool(name="psum", bufs=8))
 
@@ -42,22 +43,23 @@ def tile_picked_ccmppathbfoldd_none_po_kernel(
                 queue.dma_start(plane[32 * q : 32 * q + 4, :].bitcast(I32), src[0, 4 * q : 4 * q + 4, :].bitcast(I32))
 
         xs = keep.tile([P, T], U8, name="xs", align_bytes=64)
-        ws = keep.tile([P, S], U8, name="ws", tag="ws", align_bytes=64)
-        nc.vector.memset(xs[:].bitcast(I32), 0)
+        ws = reuse.tile([P, S], U8, name="ws", align_bytes=64, offset=4 * S - W)
+        nc.vector.memset(xs[:, :1280].bitcast(I32), 0)
+        nc.gpsimd.memset(xs[:, 1280:].bitcast(I32), 0)
         nc.vector.memset(ws[:].bitcast(I32), 0)
         l_offs = load_list("l_offs", offs)
         ww = keep.tile([P, 2 * S], U8, name="ww", tag="ww", align_bytes=64)
         nc.sync.dma_start(ww[:].bitcast(I32), w1_words[0].bitcast(I32))
+        l_ca = load_list("l_ca", ca)
         load_scale_rows(nc.sync, xs, x_scales)
         xw = keep.tile([P, T], U32, name="xw", align_bytes=64)
         nc.sync.dma_start(xw[:].bitcast(I32), x_words[0].rearrange("p n r -> p (n r)").bitcast(I32))
-        l_ca = load_list("l_ca", ca)
         load_scale_rows(nc.sync, ws, w1_scales)
+        gain = keep.tile([P, PACK], F32, name="gain")
+        nc.sync.dma_start(gain[:], gs.rearrange("(p t) o -> p (t o)", t=PACK))
         l1 = load_list("l1", n1)
         l2 = load_list("l2", n2)
         l3 = load_list("l3", n3)
-        gain = keep.tile([P, PACK], F32, name="gain")
-        nc.sync.dma_start(gain[:], gs.rearrange("(p t) o -> p (t o)", t=PACK))
         l_cb = load_list("l_cb", cb)
         l4 = load_list("l4", n4)
         l5 = load_list("l5", n5)
@@ -65,16 +67,15 @@ def tile_picked_ccmppathbfoldd_none_po_kernel(
         l7 = load_list("l7", n7)
 
         ds = [keep.tile([P, WIN], F32, name="ds%d" % t, tag="ds%d" % t, align_bytes=64) for t in range(PACK)]
-        for t in range(PACK):
-            nc.vector.memset(ds[t][:, S:], 0.0)
-        aw = [keep.tile([P, WIN], F32, name="aw%d" % t, align_bytes=64) for t in range(PACK)]
-        bw = [keep.tile([P, WIN], F32, name="bw%d" % t, align_bytes=64) for t in range(PACK)]
+        for window in ds:
+            nc.vector.memset(window[:, S:], 0.0)
+        aw = [keep.tile([P, w], F32, name="aw%d" % t, align_bytes=64) for t, w in enumerate((3 * S, 3 * S, WIN, S))]
+        bw = [keep.tile([P, w], F32, name="bw%d" % t, align_bytes=64) for t, w in enumerate((WIN, WIN, WIN, S))]
+        mixed = [aw[t // 2][:, S * (1 + t % 2) : S * (2 + t % 2)] for t in range(PACK)]
+        scratch = [bw[t % 2][:, S:] for t in range(PACK)]
 
-        def deal_words(name, src):
-            dst = keep.tile([P, S], U32, name=name, align_bytes=64)
-            nc.vector.tensor_copy(
-                dst[:].rearrange("p (t g i) -> p g t i", t=PACK, i=4), src[:].rearrange("p (g i t) -> p g t i", t=PACK, i=4)
-            )
+        def gather_dealt_words(dst, offsets):
+            nc.vector.tensor_copy(dst[:].rearrange("p (t m) -> p m t", t=PACK), xw[:].indirect(offsets[:]))
             return dst
 
         def deal_bytes(name, src):
@@ -92,48 +93,53 @@ def tile_picked_ccmppathbfoldd_none_po_kernel(
         nc.vector.tensor_copy(
             wwd[:].rearrange("p (t m b) -> p t m b", t=PACK, b=2), ww[:].rearrange("p (m t b) -> p t m b", t=PACK, b=2)
         )
-        cas = gather("cas", xs, U8, l_ca, "ww")
-        qw = gather("qw", xw, U32, l_offs, "qw")
+        cas = gather("cas", xs, U8, l_ca, "cas")
         wsd = deal_bytes("wsd", ws)
-        caw = gather("caw", xw, U32, l_ca, "ws")
+        qw = reuse.tile([P, S], U32, name="qw", align_bytes=64, offset=0)
+        nc.vector.tensor_copy(qw[:, :W], xw[:].indirect(l_offs[:, : W // 16]))
+        nc.vector.tensor_copy(qw[:, W:], xw[:].indirect(l_offs[:, W // 16 :]))
+        cawd = gather_dealt_words(reuse.tile([P, S], U32, name="cawd", align_bytes=64, offset=4 * S), l_ca)
         casd = deal_bytes("casd", cas)
-        cawd = deal_words("cawd", caw)
 
         factor = keep.tile([P, PACK], F32, name="factor")
         nc.scalar.activation(factor[:], gain[:], COPY, scale=-0.5)
 
-        for t in range(PACK):
+        for t, c0, c1 in [(0, 0, W), (0, W, S)] + [(t, 0, S) for t in range(1, PACK)]:
             acc = psum.tile([P, S], F32, name="acc")
             nc.tensor.matmul_mx(
-                out=acc[:],
+                out=acc[:, : c1 - c0],
                 lhsT=wwd[:, 2 * P * t : 2 * P * (t + 1)].bitcast(FP4X4),
                 lhsT_scale=wsd[:, P * t : P * (t + 1)],
-                rhs=qw[:].bitcast(FP8X4),
-                rhs_scale=qs[:],
+                rhs=qw[:, c0:c1].bitcast(FP8X4),
+                rhs_scale=qs[:, c0:c1],
                 start=True,
                 stop=True,
             )
-            nc.scalar.copy(ds[t][:, :S], acc[:])
+            nc.scalar.activation(ds[t][:, c0:c1], acc[:, : c1 - c0], COPY, scale=factor[:, t : t + 1])
 
         zb = keep.tile([P, S, PACK], BF16, name="zb", tag="zb", align_bytes=64)
 
-        def mix(t):
-            nc.vector.tensor_tensor(aw[t][:, S:], ds[t][:].indirect(l3[:]), bw[t][:, S:], ALU.subtract)
-            nc.scalar.activation(zb[:, :, t], aw[t][:, S:], COPY, scale=factor[:, t : t + 1])
+        def mix(t, c0, c1):
+            nc.vector.tensor_tensor(
+                mixed[t][:, c0:c1], ds[t][:].indirect(l3[:, c0 // 16 : c1 // 16]), scratch[t][:, c0:c1], ALU.subtract
+            )
+            if t % 2:
+                pair = aw[t // 2][:, S:].rearrange("p (u c) -> p c u", u=2)
+                nc.scalar.copy(zb[:, c0:c1, t - 1 : t + 1], pair[:, c0:c1, :])
 
         for t in range(PACK):
-            pa = ring.tile([P, W], F32, name="pa")
-            pb = ring.tile([P, W], F32, name="pb")
-            nc.vector.tensor_copy(pa[:], ds[t][:].indirect(l1[:]))
-            nc.vector.tensor_scalar(pb[:], ds[t][:].indirect(l2[:]), -0.5, 0.0, ALU.mult, ALU.add)
+            pa = scratch[t][:, :W]
+            pb = scratch[t][:, W:]
+            nc.vector.tensor_copy(pa, ds[t][:].indirect(l1[:]))
+            nc.vector.tensor_scalar(pb, ds[t][:].indirect(l2[:]), -0.5, 0.0, ALU.mult, ALU.add)
             if t > 0:
-                mix(t - 1)
-            nc.vector.tensor_tensor(ds[t][:].indirect(l2[:]), pa[:], pb[:], ALU.add)
-            nc.scalar.activation(bw[t][:, S:], ds[t][:, :S], COPY, scale=2.0)
-        mix(PACK - 1)
+                mix(t - 1, 0, S)
+            nc.vector.tensor_tensor(ds[t][:].indirect(l2[:]), pa, pb, ALU.add)
+            nc.scalar.activation(scratch[t], ds[t][:, :S], COPY, scale=2.0)
+        mix(PACK - 1, 0, W)
+        mix(PACK - 1, W, S)
 
-        cbw = gather("cbw", xw, U32, l_cb, "ds%d" % (PACK - 1))
-        cbwd = deal_words("cbwd", cbw)
+        cbwd = gather_dealt_words(keep.tile([P, S], U32, name="cbwd", tag="ds%d" % (PACK - 1), align_bytes=64), l_cb)
         zw = keep.tile([P, S], U32, name="zw", align_bytes=64)
         zs = keep.tile([P, S], U8, name="zs", align_bytes=64)
         nc.vector.quantize_mx(out=zw[:].bitcast(FP8X4), scales=zs[:], in_=zb[:].rearrange("p c t -> p (c t)"))
@@ -172,13 +178,13 @@ def tile_picked_ccmppathbfoldd_none_po_kernel(
                 )
                 nc.sync.dma_start(out_words[:, c0:c1], ow[:, c0:c1].bitcast(I32))
 
-        pieces = [(t, 0, S) for t in range(PACK - 1)] + [(PACK - 1, 0, W), (PACK - 1, W, S)]
+        pieces = [(t, 0, S) for t in range(PACK - 1)] + [(PACK - 1, 0, 256), (PACK - 1, 256, 384), (PACK - 1, 384, S)]
         pending = None
         for t, c0, c1 in pieces:
             n = c1 - c0
             cols = slice(c0 // 16, c1 // 16)
-            g4 = ring.tile([P, S], F32, name="g4")
-            g5 = ring.tile([P, S], F32, name="g5")
+            g4 = aw[2][:, S:] if t == 0 else ring.tile([P, S], F32, name="g4")
+            g5 = bw[2][:, S:] if t == 0 else ring.tile([P, S], F32, name="g5")
             s1 = ring.tile([P, S], F32, name="s1")
             s2 = ring.tile([P, S], F32, name="s2")
             nc.vector.tensor_copy(g4[:, :n], aw[t][:].indirect(l4[:, cols]))

@@ -1,6 +1,7 @@
 from contextlib import ExitStack
 
 import concourse.mybir as mybir
+from concourse.masks import make_identity
 
 F32 = mybir.dt.float32
 BF16 = mybir.dt.bfloat16
@@ -12,6 +13,7 @@ FP8X4 = mybir.dt.float8_e4m3fn_x4
 FP4X4 = mybir.dt.float4_e2m1fn_x4
 ALU = mybir.AluOpType
 COPY = mybir.ActivationFunctionType.Copy
+RELU = mybir.ActivationFunctionType.Relu
 
 P = 128
 PACK = 4
@@ -19,6 +21,7 @@ T = 2048
 S = 512
 W = 256
 WIN = 2 * S
+BANK = 2048
 FLOPS = 3 * 2 * 512 * 512 * 512
 
 
@@ -30,8 +33,9 @@ def tile_picked_ccmppathbfoldd_none_po_kernel(
         lists = ctx.enter_context(tc.tile_pool(name="lists", bufs=1))
         keep = ctx.enter_context(tc.tile_pool(name="keep", bufs=1))
         reuse = ctx.enter_context(tc.tile_pool(name="reuse", bufs=1))
+        turns = ctx.enter_context(tc.psum_pool(name="turns", bufs=1))
         ring = ctx.enter_context(tc.tile_pool(name="ring", bufs=2))
-        psum = ctx.enter_context(tc.psum_pool(name="psum", bufs=8))
+        psum = ctx.enter_context(tc.psum_pool(name="psum", bufs=4))
 
         def load_list(name, src):
             t = lists.tile([P, src.shape[1]], U16, name=name)
@@ -94,13 +98,15 @@ def tile_picked_ccmppathbfoldd_none_po_kernel(
             wwd[:].rearrange("p (t m b) -> p t m b", t=PACK, b=2), ww[:].rearrange("p (m t b) -> p t m b", t=PACK, b=2)
         )
         cas = gather("cas", xs, U8, l_ca, "cas")
+        casd = deal_bytes("casd", cas)
         wsd = deal_bytes("wsd", ws)
         qw = reuse.tile([P, S], U32, name="qw", align_bytes=64, offset=0)
         nc.vector.tensor_copy(qw[:, :W], xw[:].indirect(l_offs[:, : W // 16]))
         nc.vector.tensor_copy(qw[:, W:], xw[:].indirect(l_offs[:, W // 16 :]))
         cawd = gather_dealt_words(reuse.tile([P, S], U32, name="cawd", align_bytes=64, offset=4 * S), l_ca)
-        casd = deal_bytes("casd", cas)
 
+        identity = keep.tile([P, P], F32, name="identity")
+        make_identity(nc, identity[:])
         factor = keep.tile([P, PACK], F32, name="factor")
         nc.scalar.activation(factor[:], gain[:], COPY, scale=-0.5)
 
@@ -146,19 +152,22 @@ def tile_picked_ccmppathbfoldd_none_po_kernel(
         cbs = gather("cbs", xs, U8, l_cb, "zb")
         cbsd = deal_bytes("cbsd", cbs)
 
-        for t in range(PACK):
-            for words, scales, window in ((cawd, casd, aw[t]), (cbwd, cbsd, bw[t])):
-                acc = psum.tile([P, S], F32, name="acc")
-                nc.tensor.matmul_mx(
-                    out=acc[:],
-                    lhsT=words[:, P * t : P * (t + 1)].bitcast(FP8X4),
-                    lhsT_scale=scales[:, P * t : P * (t + 1)],
-                    rhs=zw[:].bitcast(FP8X4),
-                    rhs_scale=zs[:],
-                    start=True,
-                    stop=True,
-                )
-                nc.scalar.activation(window[:, :S], acc[:], COPY, scale=0.0625)
+        side_a = (cawd, casd, aw, 0.0625)
+        side_b = (cbwd, cbsd, bw, -0.0625)
+        for t0 in range(0, PACK, 2):
+            for words, scales, windows, scale in (side_a, side_b):
+                for t in (t0, t0 + 1):
+                    acc = psum.tile([P, S], F32, name="acc")
+                    nc.tensor.matmul_mx(
+                        out=acc[:],
+                        lhsT=words[:, P * t : P * (t + 1)].bitcast(FP8X4),
+                        lhsT_scale=scales[:, P * t : P * (t + 1)],
+                        rhs=zw[:].bitcast(FP8X4),
+                        rhs_scale=zs[:],
+                        start=True,
+                        stop=True,
+                    )
+                    nc.scalar.activation(windows[t][:, :S], acc[:], COPY, scale=scale)
 
         ob = keep.tile([P, S, PACK], BF16, name="ob", align_bytes=64)
         ow = keep.tile([P, S], U32, name="ow", align_bytes=64)
@@ -166,35 +175,74 @@ def tile_picked_ccmppathbfoldd_none_po_kernel(
         out_rows = out_0.rearrange("(p t) c -> p t c", t=PACK)
         out_words = out_1[0].rearrange("p c r -> p (c r)").bitcast(I32)
 
-        def finish(t, c0, c1, s1, s2):
-            n = c1 - c0
-            res = ring.tile([P, S], F32, name="res", bufs=3)
-            nc.vector.tensor_tensor(res[:, :n], s1[:, :n], s2[:, :n], ALU.max)
-            nc.scalar.copy(ob[:, c0:c1, t], res[:, :n])
-            nc.sync.dma_start(out_rows[:, t, c0:c1], res[:, :n])
-            if t == PACK - 1:
-                nc.vector.quantize_mx(
-                    out=ow[:, c0:c1].bitcast(FP8X4), scales=osc[:, c0:c1], in_=ob[:, c0:c1, :].rearrange("p c t -> p (c t)")
-                )
-                nc.sync.dma_start(out_words[:, c0:c1], ow[:, c0:c1].bitcast(I32))
+        res = [keep.tile([P, 2, S], F32, name="res%d" % u) for u in range(2)]
 
-        pieces = [(t, 0, S) for t in range(PACK - 1)] + [(PACK - 1, 0, 256), (PACK - 1, 256, 384), (PACK - 1, 384, S)]
-        pending = None
-        for t, c0, c1 in pieces:
+        def transposed_sum(bank, terms):
+            for c in range(0, S, P):
+                for k, term in enumerate(terms):
+                    nc.tensor.matmul(
+                        bank[:, c : c + P], lhsT=term[:, c : c + P], rhs=identity[:],
+                        is_transpose=True, start=(k == 0), stop=(k == len(terms) - 1),
+                    )
+
+        def fetch_a4(t, c0, c1):
+            g4 = aw[2][:, S:] if t == 0 else ring.tile([P, S], F32, name="g4")
+            nc.vector.tensor_copy(g4[:, : c1 - c0], aw[t][:].indirect(l4[:, c0 // 16 : c1 // 16]))
+            return g4
+
+        def sums(t, c0, c1, g4):
             n = c1 - c0
             cols = slice(c0 // 16, c1 // 16)
-            g4 = aw[2][:, S:] if t == 0 else ring.tile([P, S], F32, name="g4")
-            g5 = bw[2][:, S:] if t == 0 else ring.tile([P, S], F32, name="g5")
-            s1 = ring.tile([P, S], F32, name="s1")
-            s2 = ring.tile([P, S], F32, name="s2")
-            nc.vector.tensor_copy(g4[:, :n], aw[t][:].indirect(l4[:, cols]))
-            if pending is not None:
-                finish(*pending)
-            nc.vector.tensor_copy(g5[:, :n], aw[t][:].indirect(l5[:, cols]))
-            nc.vector.tensor_tensor(s1[:, :n], bw[t][:].indirect(l6[:, cols]), g4[:, :n], ALU.add)
-            nc.vector.tensor_tensor(s2[:, :n], bw[t][:].indirect(l7[:, cols]), g5[:, :n], ALU.add)
-            pending = (t, c0, c1, s1, s2)
-        finish(*pending)
+            h7 = bw[2][:, S:] if t == 0 else ring.tile([P, S], F32, name="h7")
+            minus_s1 = ring.tile([P, S], F32, name="minus_s1", bufs=3)
+            s2 = ring.tile([P, S], F32, name="s2", bufs=3)
+            nc.vector.tensor_copy(h7[:, :n], bw[t][:].indirect(l7[:, cols]))
+            nc.vector.tensor_tensor(minus_s1[:, :n], bw[t][:].indirect(l6[:, cols]), g4[:, :n], ALU.subtract)
+            nc.vector.tensor_tensor(s2[:, :n], aw[t][:].indirect(l5[:, cols]), h7[:, :n], ALU.subtract)
+            return minus_s1, s2
+
+        def round_pair(u, c0, c1):
+            nc.scalar.copy(ob[:, c0:c1, 2 * u : 2 * u + 2], res[u][:, :, c0:c1].rearrange("p u c -> p c u"))
+
+        early = [fetch_a4(t, 0, S) for t in range(2)]
+        for t in range(PACK - 1):
+            minus_s1, s2 = sums(t, 0, S, early[t] if t < 2 else fetch_a4(t, 0, S))
+            here, there = 2 * BANK * (t % 2), 2 * BANK * ((t + 1) % 2)
+            first = turns.tile([P, S], F32, name="first%d" % t, offset=here)
+            diff = turns.tile([P, S], F32, name="diff%d" % t, offset=here + BANK)
+            back = turns.tile([P, 2 * S], F32, name="back%d" % t, offset=there)
+            transposed_sum(first, [minus_s1])
+            s1_t = ring.tile([P, S], F32, name="s1_t")
+            nc.scalar.activation(s1_t[:], first[:], COPY, scale=-1.0)
+            transposed_sum(diff, [minus_s1, s2])
+            gap_t = ring.tile([P, S], F32, name="gap_t")
+            nc.scalar.activation(gap_t[:], diff[:], RELU)
+            transposed_sum(back, [s1_t, gap_t])
+            nc.scalar.copy(res[t // 2][:, t % 2, :], back[:, :S])
+            nc.sync.dma_start(out_rows[:, t, :], res[t // 2][:, t % 2, :])
+            if t == 1:
+                round_pair(0, 0, S)
+
+        pieces = [(0, 256), (256, 384), (384, S)]
+        last = PACK - 1
+        g4 = fetch_a4(last, *pieces[0])
+        for k, (c0, c1) in enumerate(pieces):
+            n = c1 - c0
+            minus_s1, s2 = sums(last, c0, c1, g4)
+            if k + 1 < len(pieces):
+                g4 = fetch_a4(last, *pieces[k + 1])
+            nc.vector.scalar_tensor_tensor(res[1][:, 1, c0:c1], minus_s1[:, :n], -1.0, s2[:, :n], ALU.mult, ALU.max)
+            round_pair(1, c0, c1)
+            if k != 1:
+                stored = slice(0, W) if k == 0 else slice(W, S)
+                nc.sync.dma_start(out_rows[:, last, stored], res[1][:, 1, stored])
+        for k, (c0, c1) in enumerate(pieces):
+            nc.vector.quantize_mx(
+                out=ow[:, c0:c1].bitcast(FP8X4), scales=osc[:, c0:c1], in_=ob[:, c0:c1, :].rearrange("p c t -> p (c t)")
+            )
+            if k != 1:
+                stored = slice(0, W) if k == 0 else slice(W, S)
+                nc.sync.dma_start(out_words[:, stored], ow[:, stored].bitcast(I32))
         for q in range(4):
             queue = nc.scalar if q % 2 else nc.sync
             queue.dma_start(out_2[0, 4 * q : 4 * q + 4, :].bitcast(I32), osc[32 * q : 32 * q + 4, :].bitcast(I32))

@@ -19,9 +19,11 @@ P = 128
 PACK = 4
 T = 2048
 S = 512
-W = 256
-WIN = 2 * S
+HALF = S // 2
+STRIPE = 16
 BANK = 2048
+XS_ON_VECTOR = 1280
+TURNED = 2
 FLOPS = 3 * 2 * 512 * 512 * 512
 
 
@@ -38,27 +40,30 @@ def tile_picked_ccmppathbfoldd_none_po_kernel(
         psum = ctx.enter_context(tc.psum_pool(name="psum", bufs=4))
 
         def load_list(name, src):
-            t = lists.tile([P, src.shape[1]], U16, name=name)
-            nc.sync.dma_start(t[:], src)
-            return t
+            tile = lists.tile([P, src.shape[1]], U16, name=name)
+            nc.sync.dma_start(tile[:], src)
+            return tile
 
-        def load_scale_rows(queue, plane, src):
+        def load_scale_rows(tile, src):
             for q in range(4):
-                queue.dma_start(plane[32 * q : 32 * q + 4, :].bitcast(I32), src[0, 4 * q : 4 * q + 4, :].bitcast(I32))
+                nc.sync.dma_start(tile[32 * q : 32 * q + 4, :].bitcast(I32), src[0, 4 * q : 4 * q + 4, :].bitcast(I32))
+
+        def entries(tile, c0, c1):
+            return tile[:, c0 // STRIPE : c1 // STRIPE]
 
         xs = keep.tile([P, T], U8, name="xs", align_bytes=64)
-        ws = reuse.tile([P, S], U8, name="ws", align_bytes=64, offset=4 * S - W)
-        nc.vector.memset(xs[:, :1280].bitcast(I32), 0)
-        nc.gpsimd.memset(xs[:, 1280:].bitcast(I32), 0)
-        nc.vector.memset(ws[:].bitcast(I32), 0)
+        w_scales = reuse.tile([P, S], U8, name="w_scales", align_bytes=64, offset=4 * S - HALF)
+        nc.vector.memset(xs[:, :XS_ON_VECTOR].bitcast(I32), 0)
+        nc.gpsimd.memset(xs[:, XS_ON_VECTOR:].bitcast(I32), 0)
+        nc.vector.memset(w_scales[:].bitcast(I32), 0)
         l_offs = load_list("l_offs", offs)
-        ww = keep.tile([P, 2 * S], U8, name="ww", tag="ww", align_bytes=64)
-        nc.sync.dma_start(ww[:].bitcast(I32), w1_words[0].bitcast(I32))
+        w_words = keep.tile([P, 2 * S], U8, name="w_words", align_bytes=64)
+        nc.sync.dma_start(w_words[:].bitcast(I32), w1_words[0].bitcast(I32))
         l_ca = load_list("l_ca", ca)
-        load_scale_rows(nc.sync, xs, x_scales)
+        load_scale_rows(xs, x_scales)
         xw = keep.tile([P, T], U32, name="xw", align_bytes=64)
         nc.sync.dma_start(xw[:].bitcast(I32), x_words[0].rearrange("p n r -> p (n r)").bitcast(I32))
-        load_scale_rows(nc.sync, ws, w1_scales)
+        load_scale_rows(w_scales, w1_scales)
         gain = keep.tile([P, PACK], F32, name="gain")
         nc.sync.dma_start(gain[:], gs.rearrange("(p t) o -> p (t o)", t=PACK))
         l1 = load_list("l1", n1)
@@ -70,16 +75,21 @@ def tile_picked_ccmppathbfoldd_none_po_kernel(
         l6 = load_list("l6", n6)
         l7 = load_list("l7", n7)
 
-        ds = [keep.tile([P, WIN], F32, name="ds%d" % t, tag="ds%d" % t, align_bytes=64) for t in range(PACK)]
+        ds = [keep.tile([P, 2 * S], F32, name="ds%d" % t, tag="ds%d" % t, align_bytes=64) for t in range(PACK)]
         for window in ds:
             nc.vector.memset(window[:, S:], 0.0)
-        aw = [keep.tile([P, w], F32, name="aw%d" % t, align_bytes=64) for t, w in enumerate((3 * S, 3 * S, WIN, S))]
-        bw = [keep.tile([P, w], F32, name="bw%d" % t, align_bytes=64) for t, w in enumerate((WIN, WIN, WIN, S))]
-        mixed = [aw[t // 2][:, S * (1 + t % 2) : S * (2 + t % 2)] for t in range(PACK)]
-        scratch = [bw[t % 2][:, S:] for t in range(PACK)]
+        a_win = [keep.tile([P, k * S], F32, name="a_win%d" % t, align_bytes=64) for t, k in enumerate((3, 3, 2, 1))]
+        b_win = [keep.tile([P, k * S], F32, name="b_win%d" % t, align_bytes=64) for t, k in enumerate((2, 2, 2, 1))]
+        z_pairs = [a_win[u][:, S:].rearrange("p (t c) -> p t c", t=2) for u in range(2)]
+        scratch = [window[:, S:] for window in (b_win[0], b_win[1], b_win[2], a_win[2])]
 
         def gather_dealt_words(dst, offsets):
             nc.vector.tensor_copy(dst[:].rearrange("p (t m) -> p m t", t=PACK), xw[:].indirect(offsets[:]))
+            return dst
+
+        def gather_scales(name, offsets, tag):
+            dst = keep.tile([P, S], U8, name=name, tag=tag, align_bytes=64)
+            nc.vector.tensor_copy(dst[:], xs[:].indirect(offsets[:]))
             return dst
 
         def deal_bytes(name, src):
@@ -87,162 +97,162 @@ def tile_picked_ccmppathbfoldd_none_po_kernel(
             nc.vector.tensor_copy(dst[:].rearrange("p (t m) -> p t m", t=PACK), src[:].rearrange("p (m t) -> p t m", t=PACK))
             return dst
 
-        def gather(name, table, dtype, offsets, tag):
-            dst = keep.tile([P, S], dtype, name=name, tag=tag, align_bytes=64)
-            nc.vector.tensor_copy(dst[:], table[:].indirect(offsets[:]))
-            return dst
+        def round_pair(dst, pair, u, c0, c1):
+            nc.scalar.copy(dst[:, c0:c1, 2 * u : 2 * u + 2], pair[:, :, c0:c1].rearrange("p t c -> p c t"))
 
-        qs = gather("qs", xs, U8, l_offs, "qs")
-        wwd = keep.tile([P, 2 * S], U8, name="wwd", align_bytes=64)
+        q_scales = gather_scales("q_scales", l_offs, "q_scales")
+        w_words_dealt = keep.tile([P, 2 * S], U8, name="w_words_dealt", align_bytes=64)
         nc.vector.tensor_copy(
-            wwd[:].rearrange("p (t m b) -> p t m b", t=PACK, b=2), ww[:].rearrange("p (m t b) -> p t m b", t=PACK, b=2)
+            w_words_dealt[:].rearrange("p (t m b) -> p t m b", t=PACK, b=2),
+            w_words[:].rearrange("p (m t b) -> p t m b", t=PACK, b=2),
         )
-        cas = gather("cas", xs, U8, l_ca, "cas")
-        casd = deal_bytes("casd", cas)
-        wsd = deal_bytes("wsd", ws)
-        qw = reuse.tile([P, S], U32, name="qw", align_bytes=64, offset=0)
-        nc.vector.tensor_copy(qw[:, :W], xw[:].indirect(l_offs[:, : W // 16]))
-        nc.vector.tensor_copy(qw[:, W:], xw[:].indirect(l_offs[:, W // 16 :]))
-        cawd = gather_dealt_words(reuse.tile([P, S], U32, name="cawd", align_bytes=64, offset=4 * S), l_ca)
+        ca_scales = deal_bytes("ca_scales", gather_scales("ca_picked", l_ca, "ca_picked"))
+        w_scales_dealt = deal_bytes("w_scales_dealt", w_scales)
+        q_words = reuse.tile([P, S], U32, name="q_words", align_bytes=64, offset=0)
+        for c0 in (0, HALF):
+            nc.vector.tensor_copy(q_words[:, c0 : c0 + HALF], xw[:].indirect(entries(l_offs, c0, c0 + HALF)))
+        ca_words = gather_dealt_words(reuse.tile([P, S], U32, name="ca_words", align_bytes=64, offset=4 * S), l_ca)
 
         identity = keep.tile([P, P], F32, name="identity")
         make_identity(nc, identity[:])
+
         factor = keep.tile([P, PACK], F32, name="factor")
         nc.scalar.activation(factor[:], gain[:], COPY, scale=-0.5)
-
-        for t, c0, c1 in [(0, 0, W), (0, W, S)] + [(t, 0, S) for t in range(1, PACK)]:
+        for t, c0, c1 in [(t, c0, c0 + HALF) for c0 in (0, HALF) for t in (1, 0)] + [(2, 0, S), (3, 0, S)]:
             acc = psum.tile([P, S], F32, name="acc")
             nc.tensor.matmul_mx(
                 out=acc[:, : c1 - c0],
-                lhsT=wwd[:, 2 * P * t : 2 * P * (t + 1)].bitcast(FP4X4),
-                lhsT_scale=wsd[:, P * t : P * (t + 1)],
-                rhs=qw[:, c0:c1].bitcast(FP8X4),
-                rhs_scale=qs[:, c0:c1],
+                lhsT=w_words_dealt[:, 2 * P * t : 2 * P * (t + 1)].bitcast(FP4X4),
+                lhsT_scale=w_scales_dealt[:, P * t : P * (t + 1)],
+                rhs=q_words[:, c0:c1].bitcast(FP8X4),
+                rhs_scale=q_scales[:, c0:c1],
                 start=True,
                 stop=True,
             )
             nc.scalar.activation(ds[t][:, c0:c1], acc[:, : c1 - c0], COPY, scale=factor[:, t : t + 1])
 
-        zb = keep.tile([P, S, PACK], BF16, name="zb", tag="zb", align_bytes=64)
+        z_bf16 = keep.tile([P, S, PACK], BF16, name="z_bf16", tag="z_bf16", align_bytes=64)
 
-        def mix(t, c0, c1):
+        def fetch_pa(t):
+            nc.vector.tensor_copy(scratch[t][:, :HALF], ds[t][:].indirect(l1[:]))
+
+        def make_z(t, c0, c1):
             nc.vector.tensor_tensor(
-                mixed[t][:, c0:c1], ds[t][:].indirect(l3[:, c0 // 16 : c1 // 16]), scratch[t][:, c0:c1], ALU.subtract
+                z_pairs[t // 2][:, t % 2, c0:c1], ds[t][:].indirect(entries(l3, c0, c1)), scratch[t][:, c0:c1], ALU.subtract
             )
             if t % 2:
-                pair = aw[t // 2][:, S:].rearrange("p (u c) -> p c u", u=2)
-                nc.scalar.copy(zb[:, c0:c1, t - 1 : t + 1], pair[:, c0:c1, :])
+                round_pair(z_bf16, z_pairs[t // 2], t // 2, c0, c1)
 
+        fetch_pa(0)
         for t in range(PACK):
-            pa = scratch[t][:, :W]
-            pb = scratch[t][:, W:]
-            nc.vector.tensor_copy(pa, ds[t][:].indirect(l1[:]))
-            nc.vector.tensor_scalar(pb, ds[t][:].indirect(l2[:]), -0.5, 0.0, ALU.mult, ALU.add)
-            if t > 0:
-                mix(t - 1, 0, S)
-            nc.vector.tensor_tensor(ds[t][:].indirect(l2[:]), pa, pb, ALU.add)
+            nc.vector.tensor_scalar(scratch[t][:, HALF:], ds[t][:].indirect(l2[:]), -0.5, 0.0, ALU.mult, ALU.add)
+            if t + 1 < PACK:
+                fetch_pa(t + 1)
+            else:
+                make_z(0, 0, S)
+            nc.vector.tensor_tensor(ds[t][:].indirect(l2[:]), scratch[t][:, :HALF], scratch[t][:, HALF:], ALU.add)
             nc.scalar.activation(scratch[t], ds[t][:, :S], COPY, scale=2.0)
-        mix(PACK - 1, 0, W)
-        mix(PACK - 1, W, S)
+        make_z(1, 0, S)
+        make_z(2, 0, S)
+        make_z(3, 0, HALF)
+        make_z(3, HALF, S)
 
-        cbwd = gather_dealt_words(keep.tile([P, S], U32, name="cbwd", tag="ds%d" % (PACK - 1), align_bytes=64), l_cb)
-        zw = keep.tile([P, S], U32, name="zw", align_bytes=64)
-        zs = keep.tile([P, S], U8, name="zs", align_bytes=64)
-        nc.vector.quantize_mx(out=zw[:].bitcast(FP8X4), scales=zs[:], in_=zb[:].rearrange("p c t -> p (c t)"))
-        cbs = gather("cbs", xs, U8, l_cb, "zb")
-        cbsd = deal_bytes("cbsd", cbs)
+        cb_words = gather_dealt_words(keep.tile([P, S], U32, name="cb_words", tag="ds3", align_bytes=64), l_cb)
+        z_words = keep.tile([P, S], U32, name="z_words", align_bytes=64)
+        z_scales = keep.tile([P, S], U8, name="z_scales", align_bytes=64)
+        nc.vector.quantize_mx(out=z_words[:].bitcast(FP8X4), scales=z_scales[:], in_=z_bf16[:].rearrange("p c t -> p (c t)"))
+        cb_scales = deal_bytes("cb_scales", gather_scales("cb_picked", l_cb, "z_bf16"))
 
-        side_a = (cawd, casd, aw, 0.0625)
-        side_b = (cbwd, cbsd, bw, -0.0625)
         for t0 in range(0, PACK, 2):
-            for words, scales, windows, scale in (side_a, side_b):
+            for words, scales, windows, scale in ((ca_words, ca_scales, a_win, 0.0625), (cb_words, cb_scales, b_win, -0.0625)):
                 for t in (t0, t0 + 1):
                     acc = psum.tile([P, S], F32, name="acc")
                     nc.tensor.matmul_mx(
                         out=acc[:],
                         lhsT=words[:, P * t : P * (t + 1)].bitcast(FP8X4),
                         lhsT_scale=scales[:, P * t : P * (t + 1)],
-                        rhs=zw[:].bitcast(FP8X4),
-                        rhs_scale=zs[:],
+                        rhs=z_words[:].bitcast(FP8X4),
+                        rhs_scale=z_scales[:],
                         start=True,
                         stop=True,
                     )
                     nc.scalar.activation(windows[t][:, :S], acc[:], COPY, scale=scale)
 
-        ob = keep.tile([P, S, PACK], BF16, name="ob", align_bytes=64)
-        ow = keep.tile([P, S], U32, name="ow", align_bytes=64)
-        osc = keep.tile([P, S], U8, name="osc", align_bytes=64)
+        out_bf16 = keep.tile([P, S, PACK], BF16, name="out_bf16", align_bytes=64)
+        out_codes = keep.tile([P, S], U32, name="out_codes", align_bytes=64)
+        out_scales = keep.tile([P, S], U8, name="out_scales", align_bytes=64)
         out_rows = out_0.rearrange("(p t) c -> p t c", t=PACK)
         out_words = out_1[0].rearrange("p c r -> p (c r)").bitcast(I32)
 
-        res = [keep.tile([P, 2, S], F32, name="res%d" % u) for u in range(2)]
+        def fetch_a4(t, c0, c1):
+            a4 = ring.tile([P, S], F32, name="a4")
+            nc.vector.tensor_copy(a4[:, : c1 - c0], a_win[t][:].indirect(entries(l4, c0, c1)))
+            return a4
+
+        def sums(t, c0, c1, a4):
+            n = c1 - c0
+            route = "turned" if t < TURNED else "direct"
+            minus_b7 = ring.tile([P, S], F32, name="minus_b7")
+            minus_s1 = ring.tile([P, S], F32, name="minus_s1_" + route)
+            s2 = ring.tile([P, S], F32, name="s2_" + route)
+            nc.vector.tensor_copy(minus_b7[:, :n], b_win[t][:].indirect(entries(l7, c0, c1)))
+            nc.vector.tensor_tensor(minus_s1[:, :n], b_win[t][:].indirect(entries(l6, c0, c1)), a4[:, :n], ALU.subtract)
+            nc.vector.tensor_tensor(s2[:, :n], a_win[t][:].indirect(entries(l5, c0, c1)), minus_b7[:, :n], ALU.subtract)
+            return minus_s1, s2
 
         def transposed_sum(bank, terms):
             for c in range(0, S, P):
                 for k, term in enumerate(terms):
                     nc.tensor.matmul(
-                        bank[:, c : c + P], lhsT=term[:, c : c + P], rhs=identity[:],
-                        is_transpose=True, start=(k == 0), stop=(k == len(terms) - 1),
+                        bank[:, c : c + P],
+                        lhsT=term[:, c : c + P],
+                        rhs=identity[:],
+                        is_transpose=True,
+                        start=(k == 0),
+                        stop=(k == len(terms) - 1),
                     )
 
-        def fetch_a4(t, c0, c1):
-            g4 = aw[2][:, S:] if t == 0 else ring.tile([P, S], F32, name="g4")
-            nc.vector.tensor_copy(g4[:, : c1 - c0], aw[t][:].indirect(l4[:, c0 // 16 : c1 // 16]))
-            return g4
-
-        def sums(t, c0, c1, g4):
-            n = c1 - c0
-            cols = slice(c0 // 16, c1 // 16)
-            h7 = bw[2][:, S:] if t == 0 else ring.tile([P, S], F32, name="h7")
-            minus_s1 = ring.tile([P, S], F32, name="minus_s1", bufs=3)
-            s2 = ring.tile([P, S], F32, name="s2", bufs=3)
-            nc.vector.tensor_copy(h7[:, :n], bw[t][:].indirect(l7[:, cols]))
-            nc.vector.tensor_tensor(minus_s1[:, :n], bw[t][:].indirect(l6[:, cols]), g4[:, :n], ALU.subtract)
-            nc.vector.tensor_tensor(s2[:, :n], aw[t][:].indirect(l5[:, cols]), h7[:, :n], ALU.subtract)
-            return minus_s1, s2
-
-        def round_pair(u, c0, c1):
-            nc.scalar.copy(ob[:, c0:c1, 2 * u : 2 * u + 2], res[u][:, :, c0:c1].rearrange("p u c -> p c u"))
-
-        early = [fetch_a4(t, 0, S) for t in range(2)]
-        for t in range(PACK - 1):
-            minus_s1, s2 = sums(t, 0, S, early[t] if t < 2 else fetch_a4(t, 0, S))
-            here, there = 2 * BANK * (t % 2), 2 * BANK * ((t + 1) % 2)
+        low_pair = keep.tile([P, 2, S], F32, name="low_pair")
+        early_a4 = [fetch_a4(t, 0, S) for t in range(TURNED)]
+        for t in range(TURNED):
+            minus_s1, s2 = sums(t, 0, S, early_a4[t])
+            here, there = 2 * BANK * t, 2 * BANK * (1 - t)
             first = turns.tile([P, S], F32, name="first%d" % t, offset=here)
             diff = turns.tile([P, S], F32, name="diff%d" % t, offset=here + BANK)
             back = turns.tile([P, 2 * S], F32, name="back%d" % t, offset=there)
             transposed_sum(first, [minus_s1])
-            s1_t = ring.tile([P, S], F32, name="s1_t")
-            nc.scalar.activation(s1_t[:], first[:], COPY, scale=-1.0)
+            s1_turned = ring.tile([P, S], F32, name="s1_turned")
+            nc.scalar.activation(s1_turned[:], first[:], COPY, scale=-1.0)
             transposed_sum(diff, [minus_s1, s2])
-            gap_t = ring.tile([P, S], F32, name="gap_t")
-            nc.scalar.activation(gap_t[:], diff[:], RELU)
-            transposed_sum(back, [s1_t, gap_t])
-            nc.scalar.copy(res[t // 2][:, t % 2, :], back[:, :S])
-            nc.sync.dma_start(out_rows[:, t, :], res[t // 2][:, t % 2, :])
-            if t == 1:
-                round_pair(0, 0, S)
+            excess = keep.tile([P, S], F32, name="excess%d" % t, tag="excess%d" % t)
+            nc.scalar.activation(excess[:], diff[:], RELU)
+            transposed_sum(back, [s1_turned, excess])
+            nc.scalar.copy(low_pair[:, t, :], back[:, :S])
+            nc.sync.dma_start(out_rows[:, t, :], low_pair[:, t, :])
+        round_pair(out_bf16, low_pair, 0, 0, S)
 
-        pieces = [(0, 256), (256, 384), (384, S)]
-        last = PACK - 1
-        g4 = fetch_a4(last, *pieces[0])
-        for k, (c0, c1) in enumerate(pieces):
+        high_pair = keep.tile([P, 2, S], F32, name="high_pair", tag="excess1")
+        quarter = S // 4
+        pieces = [(2, 0, S), (3, 0, HALF), (3, HALF, HALF + quarter), (3, HALF + quarter, S)]
+        a4 = fetch_a4(*pieces[0])
+        for k, (t, c0, c1) in enumerate(pieces):
             n = c1 - c0
-            minus_s1, s2 = sums(last, c0, c1, g4)
+            minus_s1, s2 = sums(t, c0, c1, a4)
             if k + 1 < len(pieces):
-                g4 = fetch_a4(last, *pieces[k + 1])
-            nc.vector.scalar_tensor_tensor(res[1][:, 1, c0:c1], minus_s1[:, :n], -1.0, s2[:, :n], ALU.mult, ALU.max)
-            round_pair(1, c0, c1)
-            if k != 1:
-                stored = slice(0, W) if k == 0 else slice(W, S)
-                nc.sync.dma_start(out_rows[:, last, stored], res[1][:, 1, stored])
-        for k, (c0, c1) in enumerate(pieces):
+                a4 = fetch_a4(*pieces[k + 1])
+            nc.vector.scalar_tensor_tensor(high_pair[:, t % 2, c0:c1], minus_s1[:, :n], -1.0, s2[:, :n], ALU.mult, ALU.max)
+            if t == PACK - 1:
+                round_pair(out_bf16, high_pair, 1, c0, c1)
+            nc.sync.dma_start(out_rows[:, t, c0:c1], high_pair[:, t % 2, c0:c1])
+
+        for t, c0, c1 in pieces[1:]:
             nc.vector.quantize_mx(
-                out=ow[:, c0:c1].bitcast(FP8X4), scales=osc[:, c0:c1], in_=ob[:, c0:c1, :].rearrange("p c t -> p (c t)")
+                out=out_codes[:, c0:c1].bitcast(FP8X4),
+                scales=out_scales[:, c0:c1],
+                in_=out_bf16[:, c0:c1, :].rearrange("p c t -> p (c t)"),
             )
-            if k != 1:
-                stored = slice(0, W) if k == 0 else slice(W, S)
-                nc.sync.dma_start(out_words[:, stored], ow[:, stored].bitcast(I32))
+            if c1 % HALF == 0:
+                nc.sync.dma_start(out_words[:, c1 - HALF : c1], out_codes[:, c1 - HALF : c1].bitcast(I32))
         for q in range(4):
             queue = nc.scalar if q % 2 else nc.sync
-            queue.dma_start(out_2[0, 4 * q : 4 * q + 4, :].bitcast(I32), osc[32 * q : 32 * q + 4, :].bitcast(I32))
+            queue.dma_start(out_2[0, 4 * q : 4 * q + 4, :].bitcast(I32), out_scales[32 * q : 32 * q + 4, :].bitcast(I32))

from contextlib import ExitStack

import concourse.mybir as mybir
from concourse.masks import make_identity

F32 = mybir.dt.float32
BF16 = mybir.dt.bfloat16
I32 = mybir.dt.int32
U32 = mybir.dt.uint32
U16 = mybir.dt.uint16
U8 = mybir.dt.uint8
FP8X4 = mybir.dt.float8_e4m3fn_x4
FP4X4 = mybir.dt.float4_e2m1fn_x4
ALU = mybir.AluOpType
COPY = mybir.ActivationFunctionType.Copy
RELU = mybir.ActivationFunctionType.Relu

P = 128
PACK = 4
T = 2048
S = 512
HALF = S // 2
STRIPE = 16
BANK = 2048
XS_ON_VECTOR = 1280
TURNED = 2
FLOPS = 3 * 2 * 512 * 512 * 512


def tile_picked_ccmppathbfoldd_none_po_kernel(
    tc, x_words, x_scales, w1_words, w1_scales, gs, offs, n1, n2, n3, ca, cb, n4, n5, n6, n7, out_0, out_1, out_2
):
    nc = tc.nc
    with ExitStack() as ctx:
        lists = ctx.enter_context(tc.tile_pool(name="lists", bufs=1))
        keep = ctx.enter_context(tc.tile_pool(name="keep", bufs=1))
        reuse = ctx.enter_context(tc.tile_pool(name="reuse", bufs=1))
        turns = ctx.enter_context(tc.psum_pool(name="turns", bufs=1))
        ring = ctx.enter_context(tc.tile_pool(name="ring", bufs=2))
        psum = ctx.enter_context(tc.psum_pool(name="psum", bufs=4))

        def load_list(name, src):
            tile = lists.tile([P, src.shape[1]], U16, name=name)
            nc.sync.dma_start(tile[:], src)
            return tile

        def load_scale_rows(tile, src):
            for q in range(4):
                nc.sync.dma_start(tile[32 * q : 32 * q + 4, :].bitcast(I32), src[0, 4 * q : 4 * q + 4, :].bitcast(I32))

        def entries(tile, c0, c1):
            return tile[:, c0 // STRIPE : c1 // STRIPE]

        xs = keep.tile([P, T], U8, name="xs", align_bytes=64)
        w_scales = reuse.tile([P, S], U8, name="w_scales", align_bytes=64, offset=4 * S - HALF)
        nc.vector.memset(xs[:, :XS_ON_VECTOR].bitcast(I32), 0)
        nc.gpsimd.memset(xs[:, XS_ON_VECTOR:].bitcast(I32), 0)
        nc.vector.memset(w_scales[:].bitcast(I32), 0)
        l_offs = load_list("l_offs", offs)
        w_words = keep.tile([P, 2 * S], U8, name="w_words", align_bytes=64)
        nc.sync.dma_start(w_words[:].bitcast(I32), w1_words[0].bitcast(I32))
        l_ca = load_list("l_ca", ca)
        load_scale_rows(xs, x_scales)
        xw = keep.tile([P, T], U32, name="xw", align_bytes=64)
        nc.sync.dma_start(xw[:].bitcast(I32), x_words[0].rearrange("p n r -> p (n r)").bitcast(I32))
        load_scale_rows(w_scales, w1_scales)
        gain = keep.tile([P, PACK], F32, name="gain")
        nc.sync.dma_start(gain[:], gs.rearrange("(p t) o -> p (t o)", t=PACK))
        l1 = load_list("l1", n1)
        l2 = load_list("l2", n2)
        l3 = load_list("l3", n3)
        l_cb = load_list("l_cb", cb)
        l4 = load_list("l4", n4)
        l5 = load_list("l5", n5)
        l6 = load_list("l6", n6)
        l7 = load_list("l7", n7)

        ds = [keep.tile([P, 2 * S], F32, name="ds%d" % t, tag="ds%d" % t, align_bytes=64) for t in range(PACK)]
        for window in ds:
            nc.vector.memset(window[:, S:], 0.0)
        a_win = [keep.tile([P, k * S], F32, name="a_win%d" % t, align_bytes=64) for t, k in enumerate((3, 3, 2, 1))]
        b_win = [keep.tile([P, k * S], F32, name="b_win%d" % t, align_bytes=64) for t, k in enumerate((2, 2, 2, 1))]
        z_pairs = [a_win[u][:, S:].rearrange("p (t c) -> p t c", t=2) for u in range(2)]
        scratch = [window[:, S:] for window in (b_win[0], b_win[1], b_win[2], a_win[2])]

        def gather_dealt_words(dst, offsets):
            nc.vector.tensor_copy(dst[:].rearrange("p (t m) -> p m t", t=PACK), xw[:].indirect(offsets[:]))
            return dst

        def gather_scales(name, offsets, tag):
            dst = keep.tile([P, S], U8, name=name, tag=tag, align_bytes=64)
            nc.vector.tensor_copy(dst[:], xs[:].indirect(offsets[:]))
            return dst

        def deal_bytes(name, src):
            dst = keep.tile([P, S], U8, name=name, align_bytes=64)
            nc.vector.tensor_copy(dst[:].rearrange("p (t m) -> p t m", t=PACK), src[:].rearrange("p (m t) -> p t m", t=PACK))
            return dst

        def round_pair(dst, pair, u, c0, c1):
            nc.scalar.copy(dst[:, c0:c1, 2 * u : 2 * u + 2], pair[:, :, c0:c1].rearrange("p t c -> p c t"))

        q_scales = gather_scales("q_scales", l_offs, "q_scales")
        w_words_dealt = keep.tile([P, 2 * S], U8, name="w_words_dealt", align_bytes=64)
        nc.vector.tensor_copy(
            w_words_dealt[:].rearrange("p (t m b) -> p t m b", t=PACK, b=2),
            w_words[:].rearrange("p (m t b) -> p t m b", t=PACK, b=2),
        )
        ca_scales = deal_bytes("ca_scales", gather_scales("ca_picked", l_ca, "ca_picked"))
        w_scales_dealt = deal_bytes("w_scales_dealt", w_scales)
        q_words = reuse.tile([P, S], U32, name="q_words", align_bytes=64, offset=0)
        for c0 in (0, HALF):
            nc.vector.tensor_copy(q_words[:, c0 : c0 + HALF], xw[:].indirect(entries(l_offs, c0, c0 + HALF)))
        ca_words = gather_dealt_words(reuse.tile([P, S], U32, name="ca_words", align_bytes=64, offset=4 * S), l_ca)

        identity = keep.tile([P, P], F32, name="identity")
        make_identity(nc, identity[:])

        factor = keep.tile([P, PACK], F32, name="factor")
        nc.scalar.activation(factor[:], gain[:], COPY, scale=-0.5)
        for t, c0, c1 in [(t, c0, c0 + HALF) for c0 in (0, HALF) for t in (1, 0)] + [(2, 0, S), (3, 0, S)]:
            acc = psum.tile([P, S], F32, name="acc")
            nc.tensor.matmul_mx(
                out=acc[:, : c1 - c0],
                lhsT=w_words_dealt[:, 2 * P * t : 2 * P * (t + 1)].bitcast(FP4X4),
                lhsT_scale=w_scales_dealt[:, P * t : P * (t + 1)],
                rhs=q_words[:, c0:c1].bitcast(FP8X4),
                rhs_scale=q_scales[:, c0:c1],
                start=True,
                stop=True,
            )
            nc.scalar.activation(ds[t][:, c0:c1], acc[:, : c1 - c0], COPY, scale=factor[:, t : t + 1])

        z_bf16 = keep.tile([P, S, PACK], BF16, name="z_bf16", tag="z_bf16", align_bytes=64)

        def fetch_pa(t):
            nc.vector.tensor_copy(scratch[t][:, :HALF], ds[t][:].indirect(l1[:]))

        def make_z(t, c0, c1):
            nc.vector.tensor_tensor(
                z_pairs[t // 2][:, t % 2, c0:c1], ds[t][:].indirect(entries(l3, c0, c1)), scratch[t][:, c0:c1], ALU.subtract
            )
            if t % 2:
                round_pair(z_bf16, z_pairs[t // 2], t // 2, c0, c1)

        fetch_pa(0)
        for t in range(PACK):
            nc.vector.tensor_scalar(scratch[t][:, HALF:], ds[t][:].indirect(l2[:]), -0.5, 0.0, ALU.mult, ALU.add)
            if t + 1 < PACK:
                fetch_pa(t + 1)
            else:
                make_z(0, 0, S)
            nc.vector.tensor_tensor(ds[t][:].indirect(l2[:]), scratch[t][:, :HALF], scratch[t][:, HALF:], ALU.add)
            nc.scalar.activation(scratch[t], ds[t][:, :S], COPY, scale=2.0)
        make_z(1, 0, S)
        make_z(2, 0, S)
        make_z(3, 0, HALF)
        make_z(3, HALF, S)

        cb_words = gather_dealt_words(keep.tile([P, S], U32, name="cb_words", tag="ds3", align_bytes=64), l_cb)
        z_words = keep.tile([P, S], U32, name="z_words", align_bytes=64)
        z_scales = keep.tile([P, S], U8, name="z_scales", align_bytes=64)
        nc.vector.quantize_mx(out=z_words[:].bitcast(FP8X4), scales=z_scales[:], in_=z_bf16[:].rearrange("p c t -> p (c t)"))
        cb_scales = deal_bytes("cb_scales", gather_scales("cb_picked", l_cb, "z_bf16"))

        for t0 in range(0, PACK, 2):
            for words, scales, windows, scale in ((ca_words, ca_scales, a_win, 0.0625), (cb_words, cb_scales, b_win, -0.0625)):
                for t in (t0, t0 + 1):
                    acc = psum.tile([P, S], F32, name="acc")
                    nc.tensor.matmul_mx(
                        out=acc[:],
                        lhsT=words[:, P * t : P * (t + 1)].bitcast(FP8X4),
                        lhsT_scale=scales[:, P * t : P * (t + 1)],
                        rhs=z_words[:].bitcast(FP8X4),
                        rhs_scale=z_scales[:],
                        start=True,
                        stop=True,
                    )
                    nc.scalar.activation(windows[t][:, :S], acc[:], COPY, scale=scale)

        out_bf16 = keep.tile([P, S, PACK], BF16, name="out_bf16", align_bytes=64)
        out_codes = keep.tile([P, S], U32, name="out_codes", align_bytes=64)
        out_scales = keep.tile([P, S], U8, name="out_scales", align_bytes=64)
        out_rows = out_0.rearrange("(p t) c -> p t c", t=PACK)
        out_words = out_1[0].rearrange("p c r -> p (c r)").bitcast(I32)

        def fetch_a4(t, c0, c1):
            a4 = ring.tile([P, S], F32, name="a4")
            nc.vector.tensor_copy(a4[:, : c1 - c0], a_win[t][:].indirect(entries(l4, c0, c1)))
            return a4

        def sums(t, c0, c1, a4):
            n = c1 - c0
            route = "turned" if t < TURNED else "direct"
            minus_b7 = ring.tile([P, S], F32, name="minus_b7")
            minus_s1 = ring.tile([P, S], F32, name="minus_s1_" + route)
            s2 = ring.tile([P, S], F32, name="s2_" + route)
            nc.vector.tensor_copy(minus_b7[:, :n], b_win[t][:].indirect(entries(l7, c0, c1)))
            nc.vector.tensor_tensor(minus_s1[:, :n], b_win[t][:].indirect(entries(l6, c0, c1)), a4[:, :n], ALU.subtract)
            nc.vector.tensor_tensor(s2[:, :n], a_win[t][:].indirect(entries(l5, c0, c1)), minus_b7[:, :n], ALU.subtract)
            return minus_s1, s2

        def transposed_sum(bank, terms):
            for c in range(0, S, P):
                for k, term in enumerate(terms):
                    nc.tensor.matmul(
                        bank[:, c : c + P],
                        lhsT=term[:, c : c + P],
                        rhs=identity[:],
                        is_transpose=True,
                        start=(k == 0),
                        stop=(k == len(terms) - 1),
                    )

        low_pair = keep.tile([P, 2, S], F32, name="low_pair")
        early_a4 = [fetch_a4(t, 0, S) for t in range(TURNED)]
        for t in range(TURNED):
            minus_s1, s2 = sums(t, 0, S, early_a4[t])
            here, there = 2 * BANK * t, 2 * BANK * (1 - t)
            first = turns.tile([P, S], F32, name="first%d" % t, offset=here)
            diff = turns.tile([P, S], F32, name="diff%d" % t, offset=here + BANK)
            back = turns.tile([P, 2 * S], F32, name="back%d" % t, offset=there)
            transposed_sum(first, [minus_s1])
            s1_turned = ring.tile([P, S], F32, name="s1_turned")
            nc.scalar.activation(s1_turned[:], first[:], COPY, scale=-1.0)
            transposed_sum(diff, [minus_s1, s2])
            excess = keep.tile([P, S], F32, name="excess%d" % t, tag="excess%d" % t)
            nc.scalar.activation(excess[:], diff[:], RELU)
            transposed_sum(back, [s1_turned, excess])
            nc.scalar.copy(low_pair[:, t, :], back[:, :S])
            nc.sync.dma_start(out_rows[:, t, :], low_pair[:, t, :])
        round_pair(out_bf16, low_pair, 0, 0, S)

        high_pair = keep.tile([P, 2, S], F32, name="high_pair", tag="excess1")
        quarter = S // 4
        pieces = [(2, 0, S), (3, 0, HALF), (3, HALF, HALF + quarter), (3, HALF + quarter, S)]
        a4 = fetch_a4(*pieces[0])
        for k, (t, c0, c1) in enumerate(pieces):
            n = c1 - c0
            minus_s1, s2 = sums(t, c0, c1, a4)
            if k + 1 < len(pieces):
                a4 = fetch_a4(*pieces[k + 1])
            nc.vector.scalar_tensor_tensor(high_pair[:, t % 2, c0:c1], minus_s1[:, :n], -1.0, s2[:, :n], ALU.mult, ALU.max)
            if t == PACK - 1:
                round_pair(out_bf16, high_pair, 1, c0, c1)
            nc.sync.dma_start(out_rows[:, t, c0:c1], high_pair[:, t % 2, c0:c1])

        for t, c0, c1 in pieces[1:]:
            nc.vector.quantize_mx(
                out=out_codes[:, c0:c1].bitcast(FP8X4),
                scales=out_scales[:, c0:c1],
                in_=out_bf16[:, c0:c1, :].rearrange("p c t -> p (c t)"),
            )
            if c1 % HALF == 0:
                nc.sync.dma_start(out_words[:, c1 - HALF : c1], out_codes[:, c1 - HALF : c1].bitcast(I32))
        for q in range(4):
            queue = nc.scalar if q % 2 else nc.sync
            queue.dma_start(out_2[0, 4 * q : 4 * q + 4, :].bitcast(I32), out_scales[32 * q : 32 * q + 4, :].bitcast(I32))
